import numpy as np
import ml_dtypes

BF16 = ml_dtypes.bfloat16


def bf(x):
    return np.asarray(x, np.float32).astype(BF16)


def f32(x):
    return np.asarray(x, np.float32)


def f64(x):
    return np.asarray(x).astype(np.float64)


def striped(idx):
    return np.tile(idx.reshape(-1, 16).T, (8, 1))


S, K, M, N, D, V = 512, 256, 256, 256, 4, 64


def setup_inputs():
    return {"table": bf(np.random.standard_normal((K, S))), "w": bf(np.random.standard_normal((K, M)) / np.sqrt(K)), "b": f32(0.5 * np.random.standard_normal((M, 1))), "offs": striped(np.random.permutation(S)[:N])}


def reference(table, w, b, offs):
    idx = offs[:16].T.reshape(-1)
    x = f64(table)[:, idx]
    y = f64(w).T @ x
    z = np.tanh(y + f64(b))
    return z.reshape(M, V, D).mean(axis=2)

@@ -1,0 +1,64 @@
+import concourse.mybir as mybir
+
+P = 128
+K, S = 256, 512
+M = 256
+N = 256
+D = 4
+V = N // D
+K_BLOCKS = K // P
+M_BLOCKS = M // P
+FLOPS = 2 * K * M * N
+
+BF16, F32, U16 = mybir.dt.bfloat16, mybir.dt.float32, mybir.dt.uint16
+
+
+def tile_gather_matmul_kernel(tc, table, w, b, offs, out):
+    nc = tc.nc
+    with (
+        tc.tile_pool(name="held", bufs=1) as held,
+        tc.tile_pool(name="work", bufs=2) as work,
+        tc.psum_pool(name="psum", bufs=2) as psum,
+    ):
+        offsets = held.tile([P, N // 16], U16, name="offsets")
+        nc.sync.dma_start(offsets[:], offs)
+
+        table_blocks = []
+        for k in range(K_BLOCKS):
+            block = held.tile([P, S], BF16, name="table%d" % k)
+            nc.sync.dma_start(block[:], table[k * P : (k + 1) * P, :])
+            table_blocks.append(block)
+
+        weights = held.tile([P, K_BLOCKS, M], BF16, name="weights")
+        nc.scalar.dma_start(weights[:], w.rearrange("(k p) m -> p k m", p=P))
+
+        bias = held.tile([P, M_BLOCKS], F32, name="bias")
+        with nc.allow_non_contiguous_dma(reason="one float32 to a partition"):
+            nc.scalar.dma_start(bias[:], b.rearrange("(a p) o -> p (a o)", p=P))
+
+        for a in range(M_BLOCKS):
+            bank = psum.tile([P, N], F32, name="bank")
+            for k in range(K_BLOCKS):
+                nc.tensor.matmul(
+                    bank[:],
+                    weights[:, k, a * P : (a + 1) * P],
+                    table_blocks[k][:].indirect(offsets[:]),
+                    start=(k == 0),
+                    stop=(k == K_BLOCKS - 1),
+                )
+
+            z = work.tile([P, N], F32, name="z")
+            nc.scalar.activation(
+                z[:], bank[:], mybir.ActivationFunctionType.Tanh, bias=bias[:, a : a + 1]
+            )
+
+            sums = work.tile([P, V], F32, name="sums")
+            nc.vector.tensor_reduce(
+                sums[:],
+                z[:].rearrange("p (v d) -> p v d", d=D),
+                axis=mybir.AxisListType.X,
+                op=mybir.AluOpType.add,
+            )
+            mean = work.tile([P, V], F32, name="mean")
+            nc.vector.tensor_scalar_mul(mean[:], sums[:], 1.0 / D)
+            nc.sync.dma_start(out[a * P : (a + 1) * P, :], mean[:])

@@ -9,8 +9,10 @@ V = N // D
 K_BLOCKS = K // P
 M_BLOCKS = M // P
 FLOPS = 2 * K * M * N
+WARM_MATMULS = 10
 
 BF16, F32, U16 = mybir.dt.bfloat16, mybir.dt.float32, mybir.dt.uint16
+TANH = mybir.ActivationFunctionType.Tanh
 
 
 def tile_gather_matmul_kernel(tc, table, w, b, offs, out):
@@ -18,39 +20,44 @@ def tile_gather_matmul_kernel(tc, table, w, b, offs, out):
     with (
         tc.tile_pool(name="held", bufs=1) as held,
         tc.tile_pool(name="work", bufs=2) as work,
-        tc.psum_pool(name="psum", bufs=2) as psum,
+        tc.psum_pool(name="psum", bufs=1) as psum,
     ):
         offsets = held.tile([P, N // 16], U16, name="offsets")
         nc.sync.dma_start(offsets[:], offs)
 
-        table_blocks = []
-        for k in range(K_BLOCKS):
-            block = held.tile([P, S], BF16, name="table%d" % k)
-            nc.sync.dma_start(block[:], table[k * P : (k + 1) * P, :])
-            table_blocks.append(block)
-
         weights = held.tile([P, K_BLOCKS, M], BF16, name="weights")
         nc.scalar.dma_start(weights[:], w.rearrange("(k p) m -> p k m", p=P))
 
+        table_blocks = [held.tile([P, S], BF16, name="table%d" % k) for k in range(K_BLOCKS)]
+        nc.sync.dma_start(table_blocks[0][:], table[0:P, :])
+        nc.scalar.dma_start(table_blocks[1][:], table[P : 2 * P, :])
+
         bias = held.tile([P, M_BLOCKS], F32, name="bias")
         with nc.allow_non_contiguous_dma(reason="one float32 to a partition"):
-            nc.scalar.dma_start(bias[:], b.rearrange("(a p) o -> p (a o)", p=P))
+            nc.sync.dma_start(bias[:], b.rearrange("(a p) o -> p (a o)", p=P))
 
-        for a in range(M_BLOCKS):
-            bank = psum.tile([P, N], F32, name="bank")
-            for k in range(K_BLOCKS):
+        scratch = held.tile([P, N], BF16, name="scratch")
+        nc.vector.memset(scratch[:], 0.0)
+        warm_tanh = held.tile([P, 1], F32, name="warm_tanh")
+        nc.scalar.activation(warm_tanh[:], scratch[:, 0:1], TANH)
+        warm_bank = psum.tile([P, N], F32, name="warm_bank")
+        for i in range(WARM_MATMULS):
+            nc.tensor.matmul(warm_bank[:], scratch[:, 0:P], scratch[:], start=True, stop=True)
+
+        banks = [psum.tile([P, N], F32, name="bank%d" % a) for a in range(M_BLOCKS)]
+        for k in range(K_BLOCKS):
+            for a in range(M_BLOCKS):
                 nc.tensor.matmul(
-                    bank[:],
+                    banks[a][:],
                     weights[:, k, a * P : (a + 1) * P],
                     table_blocks[k][:].indirect(offsets[:]),
                     start=(k == 0),
                     stop=(k == K_BLOCKS - 1),
                 )
 
+        for a in range(M_BLOCKS):
             z = work.tile([P, N], F32, name="z")
-            nc.scalar.activation(
-                z[:], bank[:], mybir.ActivationFunctionType.Tanh, bias=bias[:, a : a + 1]
-            )
+            nc.scalar.activation(z[:], banks[a][:], TANH, bias=bias[:, a : a + 1])
 
             sums = work.tile([P, V], F32, name="sums")
             nc.vector.tensor_reduce(

@@ -9,7 +9,6 @@ V = N // D
 K_BLOCKS = K // P
 M_BLOCKS = M // P
 FLOPS = 2 * K * M * N
-WARM_MATMULS = 10
 
 BF16, F32, U16 = mybir.dt.bfloat16, mybir.dt.float32, mybir.dt.uint16
 TANH = mybir.ActivationFunctionType.Tanh
@@ -36,13 +35,10 @@ def tile_gather_matmul_kernel(tc, table, w, b, offs, out):
         with nc.allow_non_contiguous_dma(reason="one float32 to a partition"):
             nc.sync.dma_start(bias[:], b.rearrange("(a p) o -> p (a o)", p=P))
 
-        scratch = held.tile([P, N], BF16, name="scratch")
+        scratch = held.tile([P, 1], F32, name="scratch")
         nc.vector.memset(scratch[:], 0.0)
         warm_tanh = held.tile([P, 1], F32, name="warm_tanh")
-        nc.scalar.activation(warm_tanh[:], scratch[:, 0:1], TANH)
-        warm_bank = psum.tile([P, N], F32, name="warm_bank")
-        for i in range(WARM_MATMULS):
-            nc.tensor.matmul(warm_bank[:], scratch[:, 0:P], scratch[:], start=True, stop=True)
+        nc.scalar.activation(warm_tanh[:], scratch[:], TANH)
 
         banks = [psum.tile([P, N], F32, name="bank%d" % a) for a in range(M_BLOCKS)]
         for k in range(K_BLOCKS):

@@ -33,7 +33,7 @@ def tile_gather_matmul_kernel(tc, table, w, b, offs, out):
 
         bias = held.tile([P, M_BLOCKS], F32, name="bias")
         with nc.allow_non_contiguous_dma(reason="one float32 to a partition"):
-            nc.sync.dma_start(bias[:], b.rearrange("(a p) o -> p (a o)", p=P))
+            nc.scalar.dma_start(bias[:], b.rearrange("(a p) o -> p (a o)", p=P))
 
         scratch = held.tile([P, 1], F32, name="scratch")
         nc.vector.memset(scratch[:], 0.0)

@@ -8,6 +8,7 @@ D = 4
 V = N // D
 K_BLOCKS = K // P
 M_BLOCKS = M // P
+HALVES = 2
 FLOPS = 2 * K * M * N
 
 BF16, F32, U16 = mybir.dt.bfloat16, mybir.dt.float32, mybir.dt.uint16
@@ -53,15 +54,17 @@ def tile_gather_matmul_kernel(tc, table, w, b, offs, out):
 
         for a in range(M_BLOCKS):
             z = work.tile([P, N], F32, name="z")
-            nc.scalar.activation(z[:], banks[a][:], TANH, bias=bias[:, a : a + 1])
-
             sums = work.tile([P, V], F32, name="sums")
-            nc.vector.tensor_reduce(
-                sums[:],
-                z[:].rearrange("p (v d) -> p v d", d=D),
-                axis=mybir.AxisListType.X,
-                op=mybir.AluOpType.add,
-            )
+            for h in range(HALVES):
+                entries = slice(h * N // HALVES, (h + 1) * N // HALVES)
+                nodes = slice(h * V // HALVES, (h + 1) * V // HALVES)
+                nc.scalar.activation(z[:, entries], banks[a][:, entries], TANH, bias=bias[:, a : a + 1])
+                nc.vector.tensor_reduce(
+                    sums[:, nodes],
+                    z[:, entries].rearrange("p (v d) -> p v d", d=D),
+                    axis=mybir.AxisListType.X,
+                    op=mybir.AluOpType.add,
+                )
             mean = work.tile([P, V], F32, name="mean")
             nc.vector.tensor_scalar_mul(mean[:], sums[:], 1.0 / D)
             nc.sync.dma_start(out[a * P : (a + 1) * P, :], mean[:])

@@ -42,8 +42,8 @@ def tile_gather_matmul_kernel(tc, table, w, b, offs, out):
         nc.scalar.activation(warm_tanh[:], scratch[:], TANH)
 
         banks = [psum.tile([P, N], F32, name="bank%d" % a) for a in range(M_BLOCKS)]
-        for k in range(K_BLOCKS):
-            for a in range(M_BLOCKS):
+        for a in range(M_BLOCKS):
+            for k in range(K_BLOCKS):
                 nc.tensor.matmul(
                     banks[a][:],
                     weights[:, k, a * P : (a + 1) * P],

@@ -23,18 +23,16 @@ def tile_gather_matmul_kernel(tc, table, w, b, offs, out):
         tc.psum_pool(name="psum", bufs=1) as psum,
     ):
         offsets = held.tile([P, N // 16], U16, name="offsets")
-        nc.sync.dma_start(offsets[:], offs)
-
-        weights = held.tile([P, K_BLOCKS, M], BF16, name="weights")
-        nc.scalar.dma_start(weights[:], w.rearrange("(k p) m -> p k m", p=P))
-
         table_blocks = [held.tile([P, S], BF16, name="table%d" % k) for k in range(K_BLOCKS)]
-        nc.sync.dma_start(table_blocks[0][:], table[0:P, :])
-        nc.scalar.dma_start(table_blocks[1][:], table[P : 2 * P, :])
-
+        weight_blocks = [held.tile([P, M], BF16, name="weights%d" % k) for k in range(K_BLOCKS)]
         bias = held.tile([P, M_BLOCKS], F32, name="bias")
+
+        nc.sync.dma_start(offsets[:], offs)
+        for k in range(K_BLOCKS):
+            nc.sync.dma_start(table_blocks[k][:], table[k * P : (k + 1) * P, :])
+            nc.sync.dma_start(weight_blocks[k][:], w[k * P : (k + 1) * P, :])
         with nc.allow_non_contiguous_dma(reason="one float32 to a partition"):
-            nc.scalar.dma_start(bias[:], b.rearrange("(a p) o -> p (a o)", p=P))
+            nc.sync.dma_start(bias[:], b.rearrange("(a p) o -> p (a o)", p=P))
 
         scratch = held.tile([P, 1], F32, name="scratch")
         nc.vector.memset(scratch[:], 0.0)
@@ -42,11 +40,11 @@ def tile_gather_matmul_kernel(tc, table, w, b, offs, out):
         nc.scalar.activation(warm_tanh[:], scratch[:], TANH)
 
         banks = [psum.tile([P, N], F32, name="bank%d" % a) for a in range(M_BLOCKS)]
-        for a in range(M_BLOCKS):
-            for k in range(K_BLOCKS):
+        for k in range(K_BLOCKS):
+            for a in range(M_BLOCKS):
                 nc.tensor.matmul(
                     banks[a][:],
-                    weights[:, k, a * P : (a + 1) * P],
+                    weight_blocks[k][:, a * P : (a + 1) * P],
                     table_blocks[k][:].indirect(offsets[:]),
                     start=(k == 0),
                     stop=(k == K_BLOCKS - 1),

@@ -24,27 +24,30 @@ def tile_gather_matmul_kernel(tc, table, w, b, offs, out):
     ):
         offsets = held.tile([P, N // 16], U16, name="offsets")
         table_blocks = [held.tile([P, S], BF16, name="table%d" % k) for k in range(K_BLOCKS)]
-        weight_blocks = [held.tile([P, M], BF16, name="weights%d" % k) for k in range(K_BLOCKS)]
+        weight_rows = [held.tile([P, M], BF16, name="weight_rows%d" % k) for k in range(K_BLOCKS)]
         bias = held.tile([P, M_BLOCKS], F32, name="bias")
 
         nc.sync.dma_start(offsets[:], offs)
         for k in range(K_BLOCKS):
+            nc.sync.dma_start(weight_rows[k][:], w[k * P : (k + 1) * P, :])
             nc.sync.dma_start(table_blocks[k][:], table[k * P : (k + 1) * P, :])
-            nc.sync.dma_start(weight_blocks[k][:], w[k * P : (k + 1) * P, :])
-        with nc.allow_non_contiguous_dma(reason="one float32 to a partition"):
-            nc.sync.dma_start(bias[:], b.rearrange("(a p) o -> p (a o)", p=P))
+        nc.sync.dma_start(bias[:], b.rearrange("(p a) o -> p (a o)", p=P))
 
         scratch = held.tile([P, 1], F32, name="scratch")
         nc.vector.memset(scratch[:], 0.0)
         warm_tanh = held.tile([P, 1], F32, name="warm_tanh")
         nc.scalar.activation(warm_tanh[:], scratch[:], TANH)
 
+        weight_blocks = [held.tile([P, M_BLOCKS, P], BF16, name="weights%d" % k) for k in range(K_BLOCKS)]
+        for k in range(K_BLOCKS):
+            nc.vector.tensor_copy(weight_blocks[k][:], weight_rows[k][:].rearrange("r (p a) -> r a p", a=M_BLOCKS))
+
         banks = [psum.tile([P, N], F32, name="bank%d" % a) for a in range(M_BLOCKS)]
         for k in range(K_BLOCKS):
             for a in range(M_BLOCKS):
                 nc.tensor.matmul(
                     banks[a][:],
-                    weight_blocks[k][:, a * P : (a + 1) * P],
+                    weight_blocks[k][:, a, :],
                     table_blocks[k][:].indirect(offsets[:]),
                     start=(k == 0),
                     stop=(k == K_BLOCKS - 1),
@@ -65,4 +68,4 @@ def tile_gather_matmul_kernel(tc, table, w, b, offs, out):
                 )
             mean = work.tile([P, V], F32, name="mean")
             nc.vector.tensor_scalar_mul(mean[:], sums[:], 1.0 / D)
-            nc.sync.dma_start(out[a * P : (a + 1) * P, :], mean[:])
+            nc.sync.dma_start(out.rearrange("(p a) v -> p a v", a=M_BLOCKS)[:, a, :], mean[:])

@@ -27,10 +27,11 @@ def tile_gather_matmul_kernel(tc, table, w, b, offs, out):
         weight_rows = [held.tile([P, M], BF16, name="weight_rows%d" % k) for k in range(K_BLOCKS)]
         bias = held.tile([P, M_BLOCKS], F32, name="bias")
 
+        nc.sync.dma_start(weight_rows[0][:], w[0:P, :])
         nc.sync.dma_start(offsets[:], offs)
-        for k in range(K_BLOCKS):
-            nc.sync.dma_start(weight_rows[k][:], w[k * P : (k + 1) * P, :])
-            nc.sync.dma_start(table_blocks[k][:], table[k * P : (k + 1) * P, :])
+        nc.sync.dma_start(table_blocks[0][:], table[0:P, :])
+        nc.sync.dma_start(weight_rows[1][:], w[P : 2 * P, :])
+        nc.sync.dma_start(table_blocks[1][:], table[P : 2 * P, :])
         nc.sync.dma_start(bias[:], b.rearrange("(p a) o -> p (a o)", p=P))
 
         scratch = held.tile([P, 1], F32, name="scratch")

@@ -39,16 +39,19 @@ def tile_gather_matmul_kernel(tc, table, w, b, offs, out):
         warm_tanh = held.tile([P, 1], F32, name="warm_tanh")
         nc.scalar.activation(warm_tanh[:], scratch[:], TANH)
 
-        weight_blocks = [held.tile([P, M_BLOCKS, P], BF16, name="weights%d" % k) for k in range(K_BLOCKS)]
+        weight_blocks = [
+            [held.tile([P, P], BF16, name="weights%d%d" % (k, a)) for a in range(M_BLOCKS)] for k in range(K_BLOCKS)
+        ]
         for k in range(K_BLOCKS):
-            nc.vector.tensor_copy(weight_blocks[k][:], weight_rows[k][:].rearrange("r (p a) -> r a p", a=M_BLOCKS))
+            for a in range(M_BLOCKS):
+                nc.vector.tensor_copy(weight_blocks[k][a][:], weight_rows[k][:, a:M:M_BLOCKS])
 
         banks = [psum.tile([P, N], F32, name="bank%d" % a) for a in range(M_BLOCKS)]
         for k in range(K_BLOCKS):
             for a in range(M_BLOCKS):
                 nc.tensor.matmul(
                     banks[a][:],
-                    weight_blocks[k][:, a, :],
+                    weight_blocks[k][a][:],
                     table_blocks[k][:].indirect(offsets[:]),
                     start=(k == 0),
                     stop=(k == K_BLOCKS - 1),

import concourse.mybir as mybir

P = 128
K, S = 256, 512
M = 256
N = 256
D = 4
V = N // D
K_BLOCKS = K // P
M_BLOCKS = M // P
HALVES = 2
FLOPS = 2 * K * M * N

BF16, F32, U16 = mybir.dt.bfloat16, mybir.dt.float32, mybir.dt.uint16
TANH = mybir.ActivationFunctionType.Tanh


def tile_gather_matmul_kernel(tc, table, w, b, offs, out):
    nc = tc.nc
    with (
        tc.tile_pool(name="held", bufs=1) as held,
        tc.tile_pool(name="work", bufs=2) as work,
        tc.psum_pool(name="psum", bufs=1) as psum,
    ):
        offsets = held.tile([P, N // 16], U16, name="offsets")
        table_blocks = [held.tile([P, S], BF16, name="table%d" % k) for k in range(K_BLOCKS)]
        weight_rows = [held.tile([P, M], BF16, name="weight_rows%d" % k) for k in range(K_BLOCKS)]
        bias = held.tile([P, M_BLOCKS], F32, name="bias")

        nc.sync.dma_start(weight_rows[0][:], w[0:P, :])
        nc.sync.dma_start(offsets[:], offs)
        nc.sync.dma_start(table_blocks[0][:], table[0:P, :])
        nc.sync.dma_start(weight_rows[1][:], w[P : 2 * P, :])
        nc.sync.dma_start(table_blocks[1][:], table[P : 2 * P, :])
        nc.sync.dma_start(bias[:], b.rearrange("(p a) o -> p (a o)", p=P))

        scratch = held.tile([P, 1], F32, name="scratch")
        nc.vector.memset(scratch[:], 0.0)
        warm_tanh = held.tile([P, 1], F32, name="warm_tanh")
        nc.scalar.activation(warm_tanh[:], scratch[:], TANH)

        weight_blocks = [
            [held.tile([P, P], BF16, name="weights%d%d" % (k, a)) for a in range(M_BLOCKS)] for k in range(K_BLOCKS)
        ]
        for k in range(K_BLOCKS):
            for a in range(M_BLOCKS):
                nc.vector.tensor_copy(weight_blocks[k][a][:], weight_rows[k][:, a:M:M_BLOCKS])

        banks = [psum.tile([P, N], F32, name="bank%d" % a) for a in range(M_BLOCKS)]
        for k in range(K_BLOCKS):
            for a in range(M_BLOCKS):
                nc.tensor.matmul(
                    banks[a][:],
                    weight_blocks[k][a][:],
                    table_blocks[k][:].indirect(offsets[:]),
                    start=(k == 0),
                    stop=(k == K_BLOCKS - 1),
                )

        for a in range(M_BLOCKS):
            z = work.tile([P, N], F32, name="z")
            sums = work.tile([P, V], F32, name="sums")
            for h in range(HALVES):
                entries = slice(h * N // HALVES, (h + 1) * N // HALVES)
                nodes = slice(h * V // HALVES, (h + 1) * V // HALVES)
                nc.scalar.activation(z[:, entries], banks[a][:, entries], TANH, bias=bias[:, a : a + 1])
                nc.vector.tensor_reduce(
                    sums[:, nodes],
                    z[:, entries].rearrange("p (v d) -> p v d", d=D),
                    axis=mybir.AxisListType.X,
                    op=mybir.AluOpType.add,
                )
            mean = work.tile([P, V], F32, name="mean")
            nc.vector.tensor_scalar_mul(mean[:], sums[:], 1.0 / D)
            nc.sync.dma_start(out.rearrange("(p a) v -> p a v", a=M_BLOCKS)[:, a, :], mean[:])
